import numpy as np, ml_dtypes
CORES = [8,136,40,168]
N = 4
BF = ml_dtypes.bfloat16
def gentries(a):
    return np.ascontiguousarray(a.reshape(8, 16, -1).transpose(0, 2, 1)).reshape(8, -1)
def gtable(e):
    e = np.asarray(e); return np.ascontiguousarray(e.reshape(8, -1, 16).transpose(0, 2, 1)).reshape(128, -1).astype(np.int32)
V, D, B, C = 1280, 4, 256, 512
NONE = 1 << 24
def ring(n, s, order, step):
    n[order, s] = np.roll(order, -step); n[order, s + 1] = np.roll(order, step)
def mesh(rng, pairs):
    n = np.zeros((N * V, D), np.int64); h = D // 2 - 1
    if pairs:
        q = rng.permutation(N)
        circles = [np.stack([q[i] * V + rng.permutation(B), q[i + 1] * V + rng.permutation(B)], 1).reshape(-1) for i in range(0, N, 2)]
    else:
        circles = [rng.permutation((np.arange(N)[:, None] * V + np.arange(B)).reshape(-1))]
    for o in circles:
        for i in range(h): ring(n, 2 * i, o, 2 * i + 1)
    for r in range(N):
        a = r * V + rng.permutation(B); m = r * V + B + rng.permutation(B); p = r * V + C + rng.permutation(V - C)
        ring(n, 2 * h, np.stack([a, m], 1).reshape(-1), 1)
        at = np.zeros(V - B, bool); at[rng.permutation(V - B)[:B]] = True
        o = np.zeros(V - B, np.int64); o[at] = rng.permutation(m); o[~at] = p
        for i in range(h): ring(n, 2 * i, o, i + 1)
        ring(n, 2 * h, p, h + 1)
    return rng.permuted(n, axis=1)
def planes(rng, *shape):
    p = rng.integers(np.array([-3, -3, -3, -10]), np.array([4, 4, 4, 11]), shape + (3, 4))
    return np.matmul(p.swapaxes(-1, -2), p)
def parts(rng, pairs=False):
    return planes(rng, N, 8, V), rng.integers(-15, 16, (N, 8, V, 3)), np.stack([mesh(rng, pairs) for g in range(8)])
def pack(q, c, n):
    h = np.concatenate([c, np.ones(c.shape[:-1] + (1,), c.dtype)], -1); p = h[..., :, None] * h[..., None, :]
    e = n.reshape(8, N, V, D).transpose(1, 0, 3, 2).reshape(N, 8, D * V)
    return {"qu": np.ascontiguousarray(q.transpose(0, 1, 3, 4, 2)).reshape(N, 128, V).astype(np.float32),
            "po": np.ascontiguousarray(p.transpose(0, 1, 3, 4, 2)).reshape(N, 128, V).astype(np.float32).astype(BF),
            "nb": np.stack([gtable(e[r]) for r in range(N)])}
def setup_inputs(rng):
    return pack(*parts(rng))
def setup_inputs_ties(rng):
    n = parts(rng)[2]; G = np.arange(8)[None, :, None]
    a = planes(rng, 8, 2) + np.array([1, 2])[:, None, None] * np.eye(4, dtype=np.int64); b = rng.integers(-15, 16, (8, 2, 3))
    return pack(a[G, rng.integers(0, 2, (N, 8, V))], b[G, rng.integers(0, 2, (N, 8, V))], n)
def setup_inputs_stars(rng):
    q, c, n = parts(rng); c[..., 0] = np.minimum(c[..., 0], 14)
    for g in range(8):
        m = n[g]; v = rng.permutation((np.arange(N)[:, None] * V + np.arange(B)).reshape(-1)); k = m[v]
        meet = (m[k][:, :, :, None] == k[:, None, None, :]).any((1, 2, 3)); used = np.zeros(N * V, bool); done = 0
        for w in v[~meet]:
            leaf = m[w]; near = np.concatenate([leaf, m[leaf].reshape(-1)])
            if used[near].any(): continue
            used[near] = True; done += 1
            for u in np.append(leaf, w):
                q[u // V, g, u % V] = 0; q[u // V, g, u % V, 0, 3] = q[u // V, g, u % V, 3, 0] = -499; c[u // V, g, u % V, 0] = 15 if u == w else -15
            if done == 4: break
        assert done == 4
    return pack(q, c, n)
def setup_inputs_pairs(rng):
    return pack(*parts(rng, True))
def setup_inputs_heavy(rng):
    n = np.stack([mesh(rng, False) for g in range(8)]); G = np.arange(8)[None, :, None]
    x = rng.integers(0, 9, (N, 8, V, 4, 4)); k = np.tril(x) + np.tril(x, -1).swapaxes(-1, -2)
    s = np.where(G < 4, -1, np.where(G < 6, 1, 1 - 2 * rng.integers(0, 2, (N, 8, V))))
    d = pack(s[..., None, None] * (500 - k), rng.integers(12, 16, (N, 8, V, 3)), n)
    n_all = lists_of(d["nb"]); q_all = whole_meshes(d["qu"]); p_all = whole_meshes(d["po"]); own = np.arange(N * V); large = 0
    for g in range(4):
        m1 = collapse(costs(q_all[g], p_all[g], n_all[g]), n_all[g]); q1 = q_all[g].copy()
        for i in range(D): q1 += np.where(m1[n_all[g, i]] == own, q_all[g][:, n_all[g, i]], 0)
        n2 = m1[n_all[g]]; c2 = np.where(n2 == own, NONE, costs(q1, p_all[g], n2)); m2 = collapse(c2, n2)
        large += np.count_nonzero((m1 == own) & (m2 != own) & (np.min(c2, axis=0) < -(1 << 22)))
    assert large > 0
    return d
def setup_inputs_spread(rng):
    q, c, n = parts(rng); a = (500 >> rng.integers(0, 9, (N, 8, V)))[..., None, None]
    x = rng.integers(-a, a + 1, (N, 8, V, 4, 4)); x = np.where(rng.random((N, 8, V, 1, 1)) < 0.0625, 500 - 1000 * rng.integers(0, 2, x.shape), x)
    q = np.tril(x) + np.tril(x, -1).swapaxes(-1, -2); k = rng.integers(0, 8, c.shape)
    c = np.where(k == 0, 0, np.where(k == 1, 15, np.where(k == 2, -15, c)))
    return pack(q, c, n)
def lists_of(nb):
    return np.stack([gentries(nb[r]).reshape(8, D, V) for r in range(N)], axis=2).reshape(8, D, N * V).astype(np.int64)
def whole_meshes(x):
    return x.astype(np.float64).reshape(N, 8, 16, V).transpose(1, 2, 0, 3).reshape(8, 16, N * V).astype(np.int64)
def check_inputs(d):
    bad = []; q = d["qu"].astype(np.float64).reshape(N, 8, 4, 4, V); p = d["po"].astype(np.float64).reshape(N, 8, 4, 4, V); h = p[:, :, :, 3]
    if not np.isfinite(q).all() or (q != np.rint(q)).any() or (np.abs(q) > 500).any(): bad.append("quadrics: whole numbers of size at most 500")
    if (q != q.transpose(0, 1, 3, 2, 4)).any(): bad.append("quadrics: symmetric")
    if not np.isfinite(p).all() or (h != np.rint(h)).any() or (np.abs(h) > 15).any() or (h[:, :, 3] != 1).any() or (p != h[:, :, :, None] * h[:, :, None]).any(): bad.append("points: products of whole coordinates of size at most 15 and 1")
    n = lists_of(d["nb"]).transpose(0, 2, 1); own = np.arange(N * V)[None, :, None]
    if (n < 0).any() or (n >= N * V).any(): return bad + ["neighbours: in range"]
    s = np.sort(n, axis=2)
    if (n == own).any() or (s[:, :, 1:] == s[:, :, :-1]).any(): bad.append("neighbours: different, not the vertex itself")
    if (np.sort((own * (N * V) + n).reshape(8, -1), axis=1) != np.sort((n * (N * V) + own).reshape(8, -1), axis=1)).any(): bad.append("neighbours: symmetric")
    if ((own // V != n // V) & ((own % V >= B) | (n % V >= B))).any(): bad.append("edges between ranks: columns under B")
    if ((own % V < B) & (n % V >= C)).any(): bad.append("neighbours of columns under B: columns under C")
    return bad
def costs(q, p, n):
    return np.stack([np.sum((q + q[:, n[s]]) * p[:, n[s]], axis=0) for s in range(D)])
def collapse(cost, n):
    own = np.arange(N * V); s = np.argmin(cost, axis=0)
    best = cost[s, own]; first = (best < best[n]) | ((best == best[n]) & (own < n)) | (n == own)
    return np.where(np.all(first, axis=0) & (best < NONE), n[s, own], own)
def reference(qu, po, nb):
    n_all = lists_of(nb); q_all = whole_meshes(qu); p_all = whole_meshes(po); own = np.arange(N * V)
    q1 = q_all.copy(); goal = np.zeros((8, N * V), np.int64)
    for g in range(8):
        n = n_all[g]; q = q_all[g]; p = p_all[g]
        m1 = collapse(costs(q, p, n), n)
        for s in range(D): q1[g] += np.where(m1[n[s]] == own, q[:, n[s]], 0)
        n2 = m1[n]
        m2 = collapse(np.where(n2 == own, NONE, costs(q1[g], p, n2)), n2)
        goal[g] = m2[m1]
    q1 = np.ascontiguousarray(q1.reshape(8, 16, N, V).transpose(2, 0, 1, 3)).reshape(N, 128, V)
    goal = np.ascontiguousarray(goal.reshape(8, N, V).transpose(1, 0, 2))
    return {"q1": q1.astype(np.float32), "goal": goal.astype(np.float32)}

from concourse.bass import DstId, RemoteDMATransfer
from concourse.mybir import AluOpType as A, ActivationFunctionType as F

V_, NV = 1280, 5120
f32, bf, i32, u16 = "float32", "bfloat16", "int32", "uint16"
SCRATCH = {}
for names, shape, kind in (
        ("qw", [16 + NV], f32), ("pr w s1 sd s2 g2 g3 g5", [NV], bf), ("sm prod", [NV], f32), ("qp qa pe0 go", [V_], f32), ("nbt", [4, 80], i32),
        ("nf ml tl r1 r2 r3 keep val val2 ch z rs k0 vrep vk sc", [320], f32), ("l1 l3 l4", [320], u16), ("l5", [80], u16), ("vall", [400], f32),
        ("tx", [176, 16], bf), ("tp nes e1 d fl vt", [80], f32), ("cia", [2, 256], f32), ("cib", [2, 64], f32), ("chi", [80], i32), ("dh dl", [80], bf),
        ("mk c2", [320], bf), ("idf hq", [128], f32), ("idb big dm one", [128], bf), ("bm", [144], bf), ("gm gx selc", [16], f32), ("sele seli", [16], bf),
        ("pc_i", [4], i32), ("pc_f col", [4], f32), ("o1", [16, 3], bf), ("o2 o5", [16, 2], bf), ("o3 o4", [32, 3], bf), ("x1", [48, 3], bf),
        ("x2 x5", [48, 2], bf), ("x3 x4", [96, 3], bf), ("ids", [2560], bf), ("hp", [256], bf)):
    for name in names.split():
        SCRATCH[name] = ("sbuf", [128] + shape, kind)
for names, shape, kind in (("pa pb pc pd", [2, 256], f32), ("pe pf", [512], f32), ("pw px", [1024], bf)):
    for name in names.split():
        SCRATCH[name] = ("psum", [128] + shape, kind)
BANKS = ("pa", "pb", "pc", "pd", "pe", "pf", "pw", "px")
SEMAPHORES = ["v", "s", "t", "g", "hin", "hout", "xq", "xp"] + ["d%d" % i for i in range(12)] + ["a%d" % i for i in range(6)] + ["b%d" % i for i in range(7)]
PART = {"B": (0, 256, 4096), "M": (256, 256, 3072), "R": (512, 768, 0)}
CYCLE, PECYCLE, GATHER, HAND, LOAD, HOP = 1.0e-3, 0.5e-3, 1.56, 0.18, 2.0, 5.0
CASES = ((1.04, 1.04, 1.04, 1.0, 0.16, 4.0), (0.85, 0.6, 0.86, 0.8, 0.1, 3.0), (1.2, 1.54, 1.2, 1.3, 0.25, 5.0),
         (1.0, 0.77, 1.0, 1.2, 0.25, 6.0), (1.1, 1.34, 1.1, 1.0, 0.1, 3.0), (0.9, 0.9, 0.9, 1.5, 0.2, 5.5))
TRIES = 2000
PLAN = {}


def helpers(core, cores, topo):
    return [c for c in topo.cores_of(core) if topo.die(c) != topo.die(core) and all(topo.may_write(c, d) for d in cores if d != core)][:3]


def to_peers(g, core, home, T, topo, src, dst_of, sem, local):
    n = len(T.cores)
    peers = [(T.rank_of(home) + k) % n for k in range(1, n)]
    ids = []
    for p in peers:
        rid, pid = topo.addr(T.cores[p], core)
        ids.append(DstId(rid=rid, pnc=pid))
    mask = topo.mask(core, T.cores[peers[0]])
    g.remote_dma_fused([RemoteDMATransfer(dst_ids=ids, dma_engine_mask=mask, remote_sem=sem, srcs=[src], dsts=[dst_of(p) for p in peers])], local_sem=local)


def helper_split(core, hs, topo):
    on = topo.engines(core, hs[0])
    k = len(on) // 4
    return [on[len(on) - k * (j + 1):len(on) - k * j] for j in range(3)]


def helper_program(g, core, home, j, T, topo):
    b0 = V_ * T.rank_of(home)
    other = [c for c in T.cores if c != home][0]
    g.wait_ge(T.sem.hin, len(helper_split(home, helpers(home, T.cores, topo), topo)[j]))
    if j < 2:
        to_peers(g, core, home, T, topo, T.hq[:, :], lambda p: T.qw[:, 16 + b0 + 128 * j:16 + b0 + 128 * j + 128], T.sem.xq, T.sem.hout)
    else:
        to_peers(g, core, home, T, topo, T.hp[:, :], lambda p: T.pr[:, b0 + 256:b0 + 512], T.sem.xp, T.sem.hout)
    g.wait_ge(T.sem.hout, len(topo.engines(core, other)))


def link(ops):
    state = {}
    for i, o in enumerate(ops):
        deps = set(o["after"])
        for k in o["r"] + o["w"]:
            st = state.setdefault(k, {"w": None, "r": []})
            if st["w"] is not None:
                deps.add(st["w"])
            if k in o["w"] or k in BANKS:
                deps.update(st["r"])
        deps.discard(i)
        o["deps"] = sorted(deps)
        for k in o["r"]:
            if k in BANKS:
                state[k]["r"] = [i]
            else:
                state[k]["r"].append(i)
        for k in o["w"]:
            state[k]["w"] = i
            state[k]["r"] = []


def place(ops, succ, extra, bias):
    n = len(ops)
    on = [list(o["c"])[0] for o in ops]
    rank = [0.0] * n
    for i in range(n - 1, -1, -1):
        rank[i] = min(ops[i]["c"].values()) + extra[i] + ops[i]["late"] + max([0.0] + [rank[j] + (0.0 if on[i] == on[j] == "t" else HAND) for j in succ[i]])
    busy = {e: [] for e in "vstgy"}
    start, end = [0.0] * n, [0.0] * n
    for i in sorted(range(n), key=lambda i: (-rank[i], i)):
        pick = None
        for e, c in ops[i]["c"].items():
            t = max([0.0] + [end[d] + ops[d]["late"] + (0.0 if on[d] == e == "t" else HAND) for d in ops[i]["deps"]])
            for a, b in busy.get(e, []):
                if b > t:
                    if a - t >= c:
                        break
                    t = b
            score = t + c * (1.0 + (bias[i] if e == "v" else 0.0))
            if pick is None or score < pick[0]:
                pick = (score, t, e, c)
        score, start[i], on[i], c = pick
        end[i] = start[i] + c
        if on[i] in busy:
            busy[on[i]].append((start[i], end[i]))
            busy[on[i]].sort()
    return sorted(range(n), key=lambda i: (start[i], -rank[i], i)), on


def length(ops, order, on):
    total = 0.0
    for fc, fg, ft, fl, hand, hop in CASES:
        free, end = {}, [0.0] * len(ops)
        for i in order:
            o, e = ops[i], on[i]
            c = o["c"][e]
            c = c - HOP + hop if e == "x" else c * (ft if e == "t" else fg if o["list"] else fc if o["kind"] == "c" else 1.0)
            t = 0.0 if e == "x" else free.get(e, 0.0)
            for d in o["deps"]:
                t = max(t, end[d] + ops[d]["late"] * fl + (0.0 if on[d] == e == "t" else hand))
            end[i] = free[e] = t + c
        total += max(end) / (30.0 * fc + 40.0 * fg + 40.0 * hand + 2.0 * hop)
    return total


def arrange(ops):
    if "order" not in PLAN:
        n = len(ops)
        succ = [[] for o in ops]
        for i, o in enumerate(ops):
            o["list"] = o["kind"] == "c" and any(k[:3] in ("l1.", "l3.", "l4.", "l5.") for k in o["r"])
            for d in o["deps"]:
                succ[d].append(i)
        some = [i for i in range(n) if ops[i]["e"] in "vsg"]
        both = [i for i in range(n) if len(ops[i]["c"]) > 1]
        seed = [1]

        def draw(xs):
            seed[0] = (seed[0] * 1103515245 + 12345) % 2 ** 31
            return xs[(seed[0] >> 8) % len(xs)]
        extra, bias = [0.0] * n, [0.3] * n
        best = place(ops, succ, extra, bias)
        now = length(ops, best[0], best[1])
        for k in range(TRIES):
            x, b = list(extra), list(bias)
            for j in range(draw((1, 1, 2, 3))):
                if draw((0, 1, 1)):
                    x[draw(some)] = draw((0.0, 0.0, 0.3, 1.0, 2.0, 4.0))
                else:
                    b[draw(both)] = draw((-2.0, 0.0, 0.3, 1.0, 5.0))
            got = place(ops, succ, x, b)
            new = length(ops, got[0], got[1])
            if new <= now:
                extra, bias, best, now = x, b, got, new
        PLAN["order"], PLAN["on"] = best
    for o, e in zip(ops, PLAN["on"]):
        o["e"] = e
    return PLAN["order"]


def emit(ops, eng, T):
    link(ops)
    order = arrange(ops)
    pos = {i: k for k, i in enumerate(order)}
    seen = {e: {} for e in eng}
    for i in order:
        o = ops[i]
        o["wait"] = []
        if o["f"] is None:
            continue
        far = {}
        for d in o["deps"]:
            x = ops[d]
            if x["e"] == o["e"] and (o["e"] == "t" or x["kind"] == "rem"):
                continue
            s = x["sem"] if x["kind"] != "c" else x["e"]
            if s not in far or pos[d] > pos[far[s]]:
                far[s] = d
        for s, d in far.items():
            if seen[o["e"]].get(s, -1) < pos[d]:
                seen[o["e"]][s] = pos[d]
                ops[d]["need"] = True
                o["wait"].append(d)
    count = {}
    for i in order:
        o = ops[i]
        if o["f"] is None:
            continue
        for d in o["wait"]:
            eng[o["e"]].wait_ge(T.sem[ops[d]["sem"]], ops[d]["n"])
        ins = o["f"](o["e"])
        if o["kind"] == "dma":
            ins.then_inc(T.sem[o["sem"]], 16)
        elif o["kind"] == "c" and o["need"]:
            count[o["e"]] = count.get(o["e"], 0) + 1
            o["sem"], o["n"] = o["e"], count[o["e"]]
            ins.then_inc(T.sem[o["e"]], 1)
    for o in ops:
        if o["kind"] != "c" and not o["need"]:
            eng[o["e"] if o["kind"] == "dma" else "g"].wait_ge(T.sem[o["sem"]], o["n"])


def rank_program(g, core, T, topo):
    r = T.rank_of(core)
    if r is None:
        for home in T.cores:
            hs = helpers(home, T.cores, topo)
            if core in hs:
                helper_program(g, core, home, hs.index(core), T, topo)
        return
    b0 = V_ * r
    others = [p for p in range(len(T.cores)) if p != r]
    ne = len(topo.engines(core, T.cores[others[0]]))
    V, S, P = g.vector, g.scalar, g.tensor
    eng = {"v": V, "s": S, "t": P, "g": g, "y": g.sync}
    ops = []
    nd = [0]

    def op(c, f, rd, wr, kind="c", sem=None, n=0, late=0.0, after=()):
        ops.append({"c": c, "e": list(c)[0], "f": f, "r": rd.split(), "w": wr.split(), "kind": kind, "sem": sem, "n": n, "need": False,
                    "late": late, "after": list(after)})
        return len(ops) - 1

    def dma(e, out, in_, rd, wr, late):
        op({e: 0.1}, lambda q: eng[q].dma_start(out, in_), rd, wr, "dma", "d%d" % nd[0], 16, late)
        nd[0] += 1

    def arrive(sem, n, wr, cause, late):
        op({"x": late}, None, "", wr, "x", sem, n, 0.0, [cause])

    def send(k, src, dst_of, rd, wr, late=HOP):
        i = op({"g": 0.3}, lambda q: to_peers(g, core, core, T, topo, src, dst_of, T.sem["a%d" % k], T.sem["b%d" % k]), rd, "", "rem", "b%d" % k, ne)
        arrive("a%d" % k, 3 * ne, wr, i, late)

    def share(k, n, rd):
        def at(p):
            a = n * (r - 1 if r > p else r)
            return T["x%d" % k][:, a:a + n, :]
        send(k, T["o%d" % k][:], at, rd, "x%d" % k)

    def cyc(n):
        return max(64, n) * CYCLE

    def tt(out, a, b, o, rd, wr, n=64):
        op({"v": cyc(n)}, lambda q: V.tensor_tensor(out, a, b, o), rd, wr)

    def ts(out, a, s1, o0, rd, wr, s2=None, o1=None, n=64):
        if o1 is None:
            op({"v": cyc(n)}, lambda q: V.tensor_scalar(out, a, s1, None, o0), rd, wr)
        else:
            op({"v": cyc(n)}, lambda q: V.tensor_scalar(out, a, s1, s2, o0, o1), rd, wr)

    def cp(e, out, a, rd, wr, n=64, half=False, scale=1.0):
        def f(q):
            if scale != 1.0:
                return S.activation(out, a, F.Copy, scale=scale) if q == "s" else V.tensor_scalar(out, a, scale, None, A.mult)
            return S.activation(out, a, F.Copy) if q == "s" else V.tensor_copy(out, a)
        op({q: cyc(n // 2 if half and q == "v" else n) for q in e}, f, rd, wr)

    def ms(ap, c, wr, n=64):
        op({"v": cyc(n)}, lambda q: V.memset(ap, c), "", wr)

    def mm(out, l, rr, start, stop, rd, wr, n):
        op({"t": n * PECYCLE}, lambda q: P.matmul(out, l, rr, bool(start), bool(stop)), rd, wr)

    def iota(out, pattern, base, wr, n, step=1):
        op({"g": 0.13 + 2 * n * CYCLE}, lambda q: g.iota(out, pattern, base, step, allow_small_or_imprecise_dtypes=True), "", wr)

    def scan(out, d0, d1, o0, o1, rd, wr, n):
        op({"v": cyc(n)}, lambda q: V.tensor_tensor_scan(out, d0, d1, 0.0, o0, o1), rd, wr)

    def pieces(src, rd, dst, key, i0, i1):
        t = T.tp[:, i0:i1]
        tk = " ".join("tp%d" % i for i in range(i0 // 16, i1 // 16))
        hi, mid, lo = [" ".join(k + x for k in key.split()) for x in "012"]
        c1, c2 = 1.5 * 2.0 ** 40, 1.5 * 2.0 ** 32
        ts(t, src, c2, A.add, rd, tk, -c2, A.add)
        ts(dst(0), src, c1, A.add, rd, hi, -c1, A.add)
        tt(dst(2), src, t, A.subtract, rd + " " + tk, lo, 2 * (i1 - i0))
        tt(dst(1), t, dst(0), A.subtract, tk + " " + hi, mid, 2 * (i1 - i0))

    def e3(key):
        return " ".join(k + x for k in key.split() for x in "012")

    def window(name, kind):
        t = T[name]
        if kind == "R":
            return t[:, b0 + 256:b0 + V_], "%s.M %s.R %s.S" % (name, name, name)
        if kind == "O":
            return t[:, b0:b0 + V_], "%s.B %s.M %s.R %s.S" % (name, name, name, name)
        return t[:, :], " ".join(name + x for x in (".B", ".M", ".R", ".S", ".X0", ".X1", ".X2"))

    def units(part, cut):
        n = PART[part][1]
        return [(s, x, y) for s in range(4) for x, y in (((0, cut), (cut, n)) if cut < n and (s == 3 or cut == 384) else ((0, n),))]

    def pass_on(out, name, lst, plan, sel, fields, first=False):
        for part, kind, bank, t0, last in plan:
            c0, n, off = PART[part]
            for s, x0, x1 in units(part, 512 if out == "prod" else 384):
                a = off + s * n
                wn, wk = window(name, kind)
                got = wn.indirect(T[lst][:, (a + x0) // 16:(a + x1) // 16])
                key = "%s.%s%d.%d" % (out, part, s, x0)
                wk += " %s.%s" % (lst, part)
                if out == "prod":
                    tt(T.prod[:, a + x0:a + x1], got, T.qp[:, c0 + x0:c0 + x1], A.mult, wk + " qp." + part, key, 55 + int(GATHER * (x1 - x0)))
                else:
                    cp("vs", T[out][:, a + x0:a + x1], got, wk, key, 55 + int(GATHER * (x1 - x0)))
                for x in range(x0, x1, 128):
                    y = 32 * ((c0 + x) // 128) - t0 + s
                    mm(T[bank][:, :, y:y + 29:4] if fields == 2 else T[bank][:, 0, y:y + 29:4], T[out][:, a + x:a + x + 128], T[sel][:, 0:8 * fields],
                       first, first or (last and s == 3 and x + 128 == n), key + " " + sel, bank, 256 if out == "prod" else 64)

    def to_list(src, part, bank, y, last):
        c0, n, off = PART[part]
        keys = " ".join("%s.%s%d.%d" % (src, part, s, x) for s, x, x1 in units(part, 384))
        for p in range(16):
            mm(T[bank][:, y:y + n // 4], T.bm[:, 15 - p:143 - p], T[src][:, off + p:off + 4 * n:16], False, last and p == 15, keys + " bm", bank, n // 4)

    def widen(bank, y, i0, chunks, key):
        for a in range(chunks):
            op({"t": 128 * PECYCLE}, lambda q, a=a: P.transpose(T[bank][:, y + 128 * a:y + 128 * a + 128], T.tx[:, i0 + 8 * a:i0 + 8 * a + 8, :], T.idb[:, :]), key + " idb", bank)

    def part_of(bank, a):
        t = T[bank]
        return t[:, 128 * a:128 * a + 128] if bank in ("pe", "pf") else t[:, a // 2, 128 * (a % 2):128 * (a % 2) + 128]

    def build(bank, i0, chunks, key, points, pk):
        for a in range(chunks):
            mm(part_of(bank, a), T.dm[:, :], points(a), True, False, pk + " dm", bank, 128)
            mm(part_of(bank, a), T.tx[:, i0 + 8 * a:i0 + 8 * a + 8, :], T.idb[:, :], False, True, key + " idb", bank, 128)

    def txe(i0, i1):
        return lambda i: T.tx[:, i0:i1, 4 + 5 * i]

    def own(name, a, b, pad=0):
        return T[name][:, pad + b0 + a:pad + b0 + b]

    def far(name, j, n):
        return T[name][:, V_ * others[j]:V_ * others[j] + n]

    def scaled(src, src_key, part):
        c0, n, off = PART[part]
        op({"s": cyc(n)}, lambda q: S.activation(T.qp[:, c0:c0 + n], src, F.Identity, bias=T.col[:, 2:3], scale=T.col[:, 1:2]), src_key + " col1 col2", "qp." + part)

    def choice(val, keys, halves):
        for bank, a, b, k in halves:
            tt(T.keep[:, a + 1:b], T[bank][:, 0, 1:b - a], T.r1[:, a:b - 1], A.is_ge, bank + " " + k, "keep" + bank, b - a)
        ms(T.keep[:, 0:320:4], 0.0, "keeppa keeppb", 80)
        scan(T.ch[:, :], T.keep[:, :], val, A.mult, A.max, "keeppa keeppb " + keys, "ch", 320)
        cp("v", T.chi[:, :], T.ch[:, 3:320:4], "ch", "chi", 80)
        ts(T.chi[:, :], T.chi[:, :], 8191, A.bitwise_and, "chi", "chi", n=80)
        tt(T.d[:, :], T.chi[:, :], T.vt[:, :], A.subtract, "chi vt", "d", 160)
        cp("vs", T.dh[:, :], T.d[:, :], "d", "dh", 80)
        tt(T.dl[:, :], T.d[:, :], T.dh[:, :], A.subtract, "d dh", "dl", 160)

    def fetch(k, name, row, n):
        cp("vs", T.tx[:, 80:128, row:15:5], T["x%d" % k][:], "x%d" % k, "tx.X", n, True)
        widen("px", 256, 80, 6, "tx.X")
        for j in range(3):
            cp("vs", far(name, j, 256), T.px[:, 256 + 256 * j:512 + 256 * j], "px", "%s.X%d" % (name, j), 256, True)

    LISTS = (("R", 32, 80, 0), ("M", 16, 32, 192), ("B", 0, 16, 256))
    dma("y", own("qw", 0, 256, 16), T.qu[:, 0:256], "", "qw.B", LOAD + 0.5)
    dma("s", own("pr", 0, 512), T.po[:, 0:512], "", "pr.B pr.M", LOAD + 1.0)
    dma("y", own("qw", 256, 768, 16), T.qu[:, 256:768], "", "qw.1", LOAD + 2.0)
    dma("s", own("pr", 512, V_), T.po[:, 512:V_], "", "pr.R", LOAD + 2.6)
    dma("s", T.nbt[:], T.nb[:, :], "", "nbt", LOAD + 3.2)
    dma("y", own("qw", 768, V_, 16), T.qu[:, 768:V_], "", "qw.2", LOAD + 4.0)
    op({"g": 0.14}, lambda q: g.iota(T.pc_i[:, 0:1], [[0, 1]], 0, 1), "", "pc0")
    ms(T.idf[:, :], 1.0, "idf", 128)
    ms(T.tx[:, 0:80, :], 0.0, e3("tx.B tx.M tx.R tx.S") + " tx.Bi tx.Mi tx.Bj tx.Mj", 640)
    ms(T.tx[:, 80:176, :], 0.0, "tx.X", 768)
    op({"g": 0.2}, lambda q: g.affine_select(T.gx[:, :], T.idf[:, 0:16], [[0, 2], [-16, 8]], A.is_ge, 0.0, 0, 1), "idf", "gx")
    op({"g": 0.2}, lambda q: g.affine_select(T.gm[:, :], T.gx[:, :], [[0, 2], [16, 8]], A.is_ge, 0.0, 15, -1), "gx", "gm")
    op({"g": 0.43}, lambda q: g.affine_select(T.idf[:, :], T.idf[:, :], [[-1, 128]], A.is_equal, 0.0, 0, 1), "idf", "idf")
    iota(T.vt[:, :], [[128, 10], [0, 8]], b0, "vt", 80)
    iota(T.vrep[:, :], [[128, 10], [0, 32]], b0, "vrep", 320)
    iota(T.sc[:, :], [[0, 80], [-8192, 4]], 24576, "sc", 320, 0)
    iota(T.vk[:, :], [[128, 10], [0, 8], [-8192, 4]], b0 + 24576, "vk", 320)
    for part, k0, k1, y in LISTS:
        iota(T.vall[:, y:y + 4 * (k1 - k0)], [[0, 4], [16, k1 - k0]], b0 + 16 + 16 * k0, "vall" + part, 4 * (k1 - k0))
    iota(T.vall[:, 320:400], [[16, 80]], b0 + 16, "vallO", 80)
    ts(T.pc_i[:, 1:2], T.pc_i[:, 0:1], 2, A.arith_shift_right, "pc0", "pc1", 3, A.bitwise_and)
    ts(T.pc_i[:, 2:3], T.pc_i[:, 0:1], 3, A.bitwise_and, "pc0", "pc2")
    ts(T.pc_i[:, 3:4], T.pc_i[:, 0:1], 112, A.bitwise_and, "pc0", "pc3")
    cp("v", T.pc_f[:, :], T.pc_i[:, :], "pc0 pc1 pc2 pc3", "pcf")
    ts(T.col[:, 0:1], T.pc_f[:, 2:3], T.pc_f[:, 1:2], A.subtract, "pcf", "col0", 4.0, A.add)
    ts(T.col[:, 3:4], T.col[:, 0:1], 5.0, A.min, "col0", "col3", 3.0, A.subtract)
    ts(T.col[:, 2:3], T.col[:, 0:1], 4.0, A.is_lt, "col0", "col2")
    ts(T.col[:, 1:2], T.col[:, 3:4], 0.0, A.max, "col3", "col1")
    ts(T.gx[:, :], T.gm[:, :], T.col[:, 0:1], A.mult, "gm col0", "gx")
    ts(T.dm[:, :], T.idf[:, :], T.col[:, 0:1], A.mult, "idf col0", "dm", 4.0, A.is_ge, n=128)
    cp("vs", T.idb[:, :], T.idf[:, :], "idf", "idb", 128)
    cp("vs", T.big[:, :], T.idf[:, :], "idf", "big", 128, scale=21.0 * 2 ** 20)
    ts(T.selc[:, 0:8], T.gx[:, 0:8], 3.0, A.is_ge, "gx", "selc")
    ts(T.selc[:, 8:16], T.gx[:, 0:8], 2.0, A.is_equal, "gx", "selc")
    ts(T.sele[:, :], T.gx[:, :], 3.0, A.is_equal, "gx", "sele")
    ts(T.seli[:, :], T.gx[:, :], 2.0, A.is_equal, "gx", "seli")
    ms(T.bm[:, :], 0.0, "bm")
    ts(T.bm[:, 15:143:16], T.gx[:, 0:8], 2.0, A.is_equal, "gx", "bm")
    ms(T.rs[:, :], 0.0, "rs", 320)
    ms(T.rs[:, 0:320:4], 1.0e9, "rs", 80)
    ms(T.k0[:, :], 1.0, "k0", 320)
    ms(T.k0[:, 0:320:4], 0.0, "k0", 80)
    ms(T.qw[:, 0:16], 0.0, "qw.Z")
    ms(T.one[0:1, :], 1.0, "one")
    cp("vs", T.tx[:, 0:80, 8], T.vt[:, :], "vt", "tx.Bi tx.Mi", 80)
    tt(T.tx[:, 0:80, 13], T.vt[:, :], T.tx[:, 0:80, 8], A.subtract, "vt tx.Bi", "tx.Bj tx.Mj", 160)
    ts(T.vall[:, :], T.vall[:, :], T.pc_f[:, 3:4], A.subtract, "vallR vallM vallB vallO pcf", "vall", n=400)
    for part, k0, k1, y in LISTS:
        n = 4 * (k1 - k0)
        ts(T.l1[:, y:y + n], T.nbt[:, :, k0:k1], float(-{"R": b0 + 256, "M": b0, "B": 0}[part]), A.add, "nbt", "l1." + part, n=n)
        ts(T.nf[:, y:y + n], T.nbt[:, :, k0:k1], 16.0, A.add, "nbt", "nf." + part, n=n)
    hs = helpers(core, T.cores, topo)
    split = helper_split(core, hs, topo)

    def to_helpers(q):
        trs = []
        for j in range(3):
            rid, pid = topo.addr(hs[j], core)
            src = own("qw", 128 * j, 128 * j + 128, 16) if j < 2 else own("pr", 256, 512)
            trs.append(RemoteDMATransfer(dst_ids=[DstId(rid=rid, pnc=pid)], dma_engine_mask=sum(1 << e for e in split[j]), remote_sem=T.sem.hin,
                                         srcs=[src], dsts=[T.hq[:, :] if j < 2 else T.hp[:, :]]))
        g.remote_dma_fused(trs, local_sem=T.sem.b6)
    i = op({"g": 3.0}, to_helpers, "qw.B pr.M", "first", "rem", "b6", sum(len(x) for x in split))
    arrive("xq", 6 * ne, "qw.X", i, 19.0)
    arrive("xp", 3 * ne, "pr.X", i, 19.0)
    for bank, a, b, qk, pk, eb, wb, tk, wk in (("pa", 0, 256, "qw.B", "pr.B", "pc", "pe", "tx.B", "w.B"), ("pb", 256, 768, "qw.1", "pr.M pr.R", "pd", "pf", "tx.M tx.R", "w.M w.R"),
                                               ("pa", 768, V_, "qw.2", "pr.R", "pc", "pe", "tx.S", "w.S")):
        ps = T[bank][:, 0, :] if b - a == 256 else T[bank][:]
        i0, i1 = a // 16, b // 16
        mm(ps, T.idb[:, :], own("pr", a, b), True, True, "idb " + pk, bank, b - a)
        tt(T.pe0[:, a:b], ps, own("qw", a, b, 16), A.mult, bank + " " + qk, "pe0.%d" % a, b - a)
        for x in range((b - a) // 128):
            mm(T[eb][:, 0, 8 * x:8 * x + 8], T.pe0[:, a + 128 * x:a + 128 * x + 128], T.gm[:, 0:8], True, True, "pe0.%d gm" % a, eb, 256)
        pieces(T[eb][:, 0, 0:i1 - i0], eb, txe(i0, i1), tk, i0, i1)
        cp("s", T.nes[:, i0:i1], T[eb][:, 0, 0:i1 - i0], eb, "nes.a" if a else "nes.b", scale=-1.0)
        build(wb, i0, (b - a) // 128, e3(tk) + " tx.Bi tx.Bj", lambda x, a=a: own("pr", a + 128 * x, a + 128 * x + 128), pk)
        cp("vs", own("w", a, b), T[wb][:, 0:b - a], wb, wk, b - a)
        if a == 0:
            send(0, own("w", 0, 256), lambda p: own("w", 0, 256), "w.B first", "w.X0 w.X1 w.X2", HOP + 3.0)
    for part, k in (("B", "qw.B"), ("M", "qw.1"), ("R", "qw.1 qw.2")):
        c0, n, off = PART[part]
        scaled(own("qw", c0, c0 + n, 16), k, part)
        cp("s", T.qa[:, c0:c0 + n], own("qw", c0, c0 + n, 16), k, "qa." + part, n)
    for s in range(4):
        cp("s", T.cia[:, 1, s:256:4], T.nes[:, 16:80], "nes.a", "cia.e%d" % s)
        cp("s", T.cib[:, 1, s:64:4], T.nes[:, 0:16], "nes.b", "cib.e%d" % s)
    pass_on("prod", "w", "l1", (("R", "R", "pa", 64, 0), ("M", "O", "pa", 64, 0), ("B", "A", "pb", 0, 0)), "selc", 2, True)
    scan(T.r1[:, 64:320], T.rs[:, 64:320], T.pa[:, 0, :], A.add, A.min, "rs pa", "r1.M r1.R", 256)
    pieces(T.r1[:, 67:320:4], "r1.M r1.R", txe(16, 80), "tx.M tx.R tx.S", 16, 80)
    widen("pw", 0, 16, 8, e3("tx.M tx.R") + " tx.Mi tx.Mj")
    cp("vs", own("s1", 256, V_), T.pw[:, :], "pw", "s1.M s1.R s1.S", 1024, True)
    tt(T.cia[:, 0, :], T.pa[:, 1, :], T.vrep[:, 64:320], A.is_gt, "pa vrep", "cia.c", 256)
    tt(T.val[:, 64:320], T.pa[:, 1, :], T.sc[:, 64:320], A.add, "pa sc", "val.a", 256)
    scan(T.r1[:, 0:64], T.rs[:, 0:64], T.pb[:, 0, 0:64], A.add, A.min, "rs pb", "r1.B", 64)
    pieces(T.r1[:, 3:64:4], "r1.B", lambda i: T.o1[:, :, i], "o1", 0, 16)
    share(1, 16, e3("o1"))
    tt(T.cib[:, 0, :], T.pb[:, 1, 0:64], T.vrep[:, 0:64], A.is_gt, "pb vrep", "cib.c")
    tt(T.val[:, 0:64], T.pb[:, 1, 0:64], T.sc[:, 0:64], A.add, "pb sc", "val.b")
    cp("vs", T.tx[:, 0:16, 4:15:5], T.o1[:], e3("o1"), e3("tx.B"))
    widen("px", 0, 0, 2, e3("tx.B") + " tx.Bi tx.Bj")
    cp("vs", own("s1", 0, 256), T.px[:, 0:256], "px", "s1.B", 256, True)
    fetch(1, "s1", 4, 144)
    choice(T.val[:, :], "val.a val.b", (("pa", 64, 320, "r1.M r1.R"), ("pb", 0, 64, "r1.B")))
    mm(T.pc[:], T.idf[:, :], T.cia[:], True, False, "idf cia.c cia.e0 cia.e1 cia.e2 cia.e3", "pc", 2048)
    mm(T.pd[:, :, 0:64], T.idf[:, :], T.cib[:], True, False, "idf cib.c cib.e0 cib.e1 cib.e2 cib.e3", "pd", 512)
    pass_on("g2", "s1", "l1", (("R", "R", "pc", 64, 0), ("M", "O", "pc", 64, 1), ("B", "A", "pd", 0, 1)), "sele", 2)
    scan(T.r2[:, 64:320], T.rs[:, 64:320], T.pc[:, 0, :], A.add, A.min, "rs pc", "r2.a", 256)
    tt(T.fl[:, 16:80], T.r1[:, 67:320:4], T.r2[:, 67:320:4], A.is_lt, "r1.M r1.R r2.a", "fl.a", 128)
    tt(T.tx[:, 16:80, 8], T.fl[:, 16:80], T.dh[:, 16:80], A.mult, "fl.a dh", "tx.Mi", 128)
    tt(T.tx[:, 16:80, 13], T.fl[:, 16:80], T.dl[:, 16:80], A.mult, "fl.a dl", "tx.Mj", 128)
    widen("pw", 0, 16, 8, e3("tx.M tx.R") + " tx.Mi tx.Mj")
    cp("vs", own("sd", 256, V_), T.pw[:, :], "pw", "sd.M sd.R sd.S", 1024, True)
    scan(T.r2[:, 0:64], T.rs[:, 0:64], T.pd[:, 0, 0:64], A.add, A.min, "rs pd", "r2.b", 64)
    tt(T.fl[:, 0:16], T.r1[:, 3:64:4], T.r2[:, 3:64:4], A.is_lt, "r1.B r2.b", "fl.b")
    tt(T.o2[:, :, 0], T.fl[:, 0:16], T.dh[:, 0:16], A.mult, "fl.b dh", "o2a")
    tt(T.o2[:, :, 1], T.fl[:, 0:16], T.dl[:, 0:16], A.mult, "fl.b dl", "o2b")
    share(2, 16, "o2a o2b")
    cp("vs", T.tx[:, 0:16, 8:14:5], T.o2[:], "o2a o2b", "tx.Bi tx.Bj")
    widen("px", 0, 0, 2, e3("tx.B") + " tx.Bi tx.Bj")
    cp("vs", own("sd", 0, 256), T.px[:, 0:256], "px", "sd.B", 256, True)
    fetch(2, "sd", 8, 96)
    mm(T.pa[:, 0, :], T.idf[:, :], T.val[:, 64:320], True, False, "idf val.a", "pa", 1024)
    mm(T.pe[:, 256:512], T.idf[:, :], T.nf[:, 0:256], True, True, "idf nf.R nf.M", "pe", 1024)
    mm(T.pe[:, 0:256], T.idf[:, :], T.nf[:, 0:256], True, False, "idf nf.R nf.M", "pe", 1024)
    mm(T.pb[:, 0, 0:64], T.idf[:, :], T.val[:, 0:64], True, False, "idf val.b", "pb", 256)
    mm(T.pf[:, 0:64], T.idf[:, :], T.nf[:, 256:320], True, False, "idf nf.B", "pf", 256)
    pass_on("g3", "sd", "l1", (("R", "R", "pa", 64, 0), ("M", "O", "pa", 64, 1), ("B", "A", "pb", 0, 1)), "seli", 1)
    for part, lb, y in (("R", "pe", 0), ("M", "pe", 192), ("B", "pf", 0)):
        to_list("g3", part, lb, y, part != "R")
    for bank, a, b, k in (("pe", 0, 256, "l3.R l3.M"), ("pf", 256, 320, "l3.B")):
        tt(T.ml[:, a:b], T[bank][:, 0:b - a], T.vall[:, a:b], A.is_equal, bank + " vall", "ml" + bank, b - a)
        tt(T.tl[:, a:b], T.ml[:, a:b], T.nf[:, a:b] if a else T.pe[:, 256:512], A.mult, "ml%s %s" % (bank, "nf.B" if a else "pe"), "tl" + bank, 128 if a else 256)
        cp("v", T.l3[:, a:b], T.tl[:, a:b], "tl" + bank, k, b - a)
    ts(T.l4[:, 0:192], T.pe[:, 0:192], float(-16 - b0), A.add, "pe", "l4.R", n=192)
    ts(T.l4[:, 192:256], T.pe[:, 192:256], -16.0, A.add, "pe", "l4.M")
    ts(T.l4[:, 256:320], T.pf[:, 0:64], -16.0, A.add, "pf", "l4.B")
    for bank, ybank, a, b, k in (("pa", "pc", 64, 320, "a"), ("pb", "pd", 0, 64, "b")):
        tt(T.mk[:, a:b], T[bank][:, 0, 0:b - a], T.vk[:, a:b], A.is_equal, bank + " vk", "mk." + k, b - a)
        tt(T.z[:, a:b], T[ybank][:, 1, 0:b - a], T.mk[:, a:b], A.mult, ybank + " mk." + k, "z." + k, b - a)
        scan(T.r3[:, a:b], T.k0[:, a:b], T.z[:, a:b], A.mult, A.add, "k0 z." + k, "r3." + k, b - a)
        tt(T.c2[:, a:b], T[bank][:, 0, 0:b - a], T.vk[:, a:b], A.is_ge, bank + " vk", "c2." + k, b - a)
        cp("vs", T.val2[:, a:b], T[bank][:, 0, 0:b - a], bank, "val2." + k, b - a)
    tt(T.e1[:, 0:32], T.r3[:, 3:128:4], T.nes[:, 0:32], A.subtract, "r3.a r3.b nes.a nes.b", "e1.C")
    tt(T.e1[:, 32:80], T.r3[:, 131:320:4], T.nes[:, 32:80], A.subtract, "r3.a nes.a", "e1.R", 96)
    pieces(T.e1[:, 0:32], "e1.C", lambda i: T.o3[:, :, i], "o3", 0, 32)
    share(3, 32, e3("o3"))
    cp("vs", T.tx[:, 0:32, 4:15:5], T.o3[:], e3("o3"), e3("tx.B tx.M"), 96, True)
    pieces(T.e1[:, 32:80], "e1.R", txe(32, 80), "tx.R", 32, 80)
    mm(T.pf[:, 64:144], T.idf[:, :], T.vall[:, 320:400], True, False, "idf vall", "pf", 320)
    for p in range(16):
        mm(T.pf[:, 64:144], T.bm[:, 15 - p:143 - p], T.sd[:, b0 + p:b0 + V_:16], False, p == 15, "bm sd.B sd.M sd.R", "pf", 80)
    ts(T.l5[:, 0:16], T.pf[:, 64:80], -16.0, A.add, "pf", "l5.B")
    ts(T.l5[:, 16:80], T.pf[:, 80:144], float(-16 - b0), A.add, "pf", "l5.R")
    iota(T.ids[0:1, 0:V_], [[64, 20], [0, 64]], b0, "ids", V_)
    for j in range(3):
        iota(T.ids[0:1, V_ + 256 * j:V_ + 256 * j + 256], [[64, 4], [0, 64]], V_ * others[j], "ids", 256)
    iota(T.ids[0:1, 2048:2560], [[0, 8], [1, 64]], 0, "ids", 512)
    build("pc", 32, 4, e3("tx.R") + " tx.Mi tx.Mj", lambda a: own("pr", 512 + 128 * a, 640 + 128 * a), "pr.R")
    cp("s", own("w", 512, 1024), T.pc[:], "pc", "w.R w.S", 512)
    build("pe", 64, 2, e3("tx.R") + " tx.Mi tx.Mj", lambda a: own("pr", 1024 + 128 * a, 1152 + 128 * a), "pr.R")
    cp("s", own("w", 1024, V_), T.pe[:, 0:256], "pe", "w.S", 256)
    build("pd", 0, 4, e3("tx.B tx.M") + " tx.Bi tx.Bj tx.Mi tx.Mj", lambda a: own("pr", 128 * a, 128 * a + 128), "pr.B pr.M")
    cp("s", own("w", 0, 512), T.pd[:], "pd", "w.B w.M", 512)
    cp("s", T.tx[:, 80:176, 4:15:5], T.x3[:], "x3", "tx.X", 288)
    for j in range(3):
        bank = ("pc", "pd", "pe")[j]
        build(bank, 80 + 32 * j, 4, "tx.X", lambda a, j=j: far("w" if a < 2 else "pr", j, 512)[:, 128 * a:128 * a + 128], "w.X%d pr.X" % j)
        cp("s", far("w", j, 512), T[bank][:], bank, "w.X%d" % j, 512)
    for part in "RMB":
        c0, n, off = PART[part]
        for s in range(4):
            a = off + s * n
            tt(T.qa[:, c0:c0 + n], T.qw[:, :].indirect(T.l3[:, a // 16:(a + n) // 16]), T.qa[:, c0:c0 + n], A.add,
               "qw.Z qw.B qw.1 qw.2 qw.X l3.%s qa.%s" % (part, part), "qa." + part, 55 + int(GATHER * n))
        scaled(T.qa[:, c0:c0 + n], "qa." + part, part)
    dma("y", T.q1[:, 512:V_], T.qa[:, 512:V_], "qa.R", "", LOAD + 2.0)
    dma("y", T.q1[:, 0:512], T.qa[:, 0:512], "qa.M qa.B", "", LOAD + 2.0)
    mm(T.pb[:, 0, 0:192], T.big[:, :], T.mk[:, 128:320], True, False, "big mk.a", "pb", 192)
    mm(T.pa[:, 0, 0:128], T.big[:, :], T.mk[:, 0:128], True, False, "big mk.a mk.b", "pa", 128)
    pass_on("prod", "w", "l4", (("R", "O", "pb", 128, 1), ("M", "A", "pa", 0, 0), ("B", "A", "pa", 0, 1)), "selc", 1)
    scan(T.r1[:, 0:128], T.rs[:, 0:128], T.pa[:, 0, 0:128], A.add, A.min, "rs pa", "r1.B r1.M", 128)
    pieces(T.r1[:, 3:128:4], "r1.B r1.M", lambda i: T.o4[:, :, i], "o4", 0, 32)
    share(4, 32, e3("o4"))
    cp("vs", T.tx[:, 0:32, 4:15:5], T.o4[:], e3("o4"), e3("tx.B tx.M"), 96, True)
    widen("px", 0, 0, 4, e3("tx.B tx.M"))
    cp("vs", own("s2", 0, 512), T.px[:, 0:512], "px", "s2.B s2.M", 512, True)
    scan(T.r1[:, 128:320], T.rs[:, 128:320], T.pb[:, 0, 0:192], A.add, A.min, "rs pb", "r1.R", 192)
    pieces(T.r1[:, 131:320:4], "r1.R", txe(32, 80), "tx.R", 32, 80)
    widen("pw", 0, 32, 6, e3("tx.R"))
    cp("vs", own("s2", 512, V_), T.pw[:, 0:768], "pw", "s2.R s2.S", 768, True)
    cp("vs", T.tx[:, 80:176, 4:15:5], T.x4[:], "x4", "tx.X", 288, True)
    widen("px", 0, 80, 8, "tx.X")
    widen("pw", 0, 144, 4, "tx.X")
    cp("vs", far("s2", 0, 512), T.px[:, 0:512], "px", "s2.X0", 512, True)
    cp("vs", far("s2", 2, 512), T.pw[:, 0:512], "pw", "s2.X2", 512, True)
    cp("vs", far("s2", 1, 512), T.px[:, 512:1024], "px", "s2.X1", 512, True)
    choice(T.val2[:, :], "val2.a val2.b", (("pa", 0, 128, "r1.B r1.M"), ("pb", 128, 320, "r1.R")))
    mm(T.pd[:, 0, 0:64], T.idb[:, :], T.c2[:, 0:64], True, False, "idb c2.b", "pd", 64)
    mm(T.pc[:, 0, :], T.idb[:, :], T.c2[:, 64:320], True, False, "idb c2.a", "pc", 256)
    pass_on("g5", "s2", "l4", (("R", "O", "pc", 64, 0), ("M", "A", "pc", 64, 1), ("B", "A", "pd", 0, 1)), "sele", 1)

    def spread(bank, x, chunks, key):
        for a in range(chunks):
            for i in range(2):
                mm(part_of(bank, a), T.g3[:, x + 128 * a + i:x + 128 * a + i + 128], T.idb[:, :], False, i == 1 and a == chunks - 1, key + " idb", bank, 128)
    scan(T.r2[:, 0:64], T.rs[:, 0:64], T.pd[:, 0, 0:64], A.add, A.min, "rs pd", "r2.b", 64)
    for bank, ps, a, b in (("pa", T.pa[:, 0, :], 0, 256), ("pe", T.pe[:, :], 256, 768), ("pf", T.pf[:, :], 768, V_), ("pb", T.pb[:], V_, V_ + 512), ("pd", T.pd[:, 0, :], V_ + 512, 2048)):
        mm(ps, T.one[0:1, :], T.ids[0:1, a:b], True, False, "one ids", bank, b - a)
        mm(ps, T.one[0:1, :], T.ids[0:1, 2048:2048 + b - a], False, False, "one ids", bank, b - a)
    tt(T.fl[:, 0:16], T.r1[:, 3:64:4], T.r2[:, 3:64:4], A.is_lt, "r1.B r2.b", "fl.b")
    tt(T.o5[:, :, 0], T.fl[:, 0:16], T.dh[:, 0:16], A.mult, "fl.b dh", "o5a")
    tt(T.o5[:, :, 1], T.fl[:, 0:16], T.dl[:, 0:16], A.mult, "fl.b dl", "o5b")
    share(5, 16, "o5a o5b")
    for i in range(2):
        cp("vs", T.g3[:, i:256:16], T.o5[:, :, i], "o5a o5b", "tf.B%d" % i)
        cp("vs", T.g3[:, 1408 + i:2176:16], T.x5[:, :, i], "x5 dh", "tf.X%d" % i)
    spread("pa", 0, 2, "tf.B0 tf.B1")
    cp("vs", own("sm", 0, 256), T.pa[:, 0, :], "pa", "sm.B", 256)
    scan(T.r2[:, 64:320], T.rs[:, 64:320], T.pc[:, 0, :], A.add, A.min, "rs pc", "r2.a", 256)
    tt(T.fl[:, 16:80], T.r1[:, 67:320:4], T.r2[:, 67:320:4], A.is_lt, "r1.M r1.R r2.a", "fl.a", 128)
    tt(T.g3[:, 272:1296:16], T.fl[:, 16:80], T.dh[:, 16:80], A.mult, "fl.a dh", "tf.M0", 128)
    tt(T.g3[:, 273:1296:16], T.fl[:, 16:80], T.dl[:, 16:80], A.mult, "fl.a dl", "tf.M1", 128)
    spread("pe", 272, 4, "tf.M0 tf.M1")
    spread("pf", 784, 4, "tf.M0 tf.M1")
    cp("vs", own("sm", 256, 768), T.pe[:, :], "pe", "sm.M sm.R", 512)
    cp("vs", own("sm", 768, V_), T.pf[:, :], "pf", "sm.S", 512)
    spread("pb", 1408, 4, "tf.X0 tf.X1")
    spread("pd", 1920, 2, "tf.X0 tf.X1")
    for j in range(3):
        cp("vs", far("sm", j, 256), T.pb[:, j, :] if j < 2 else T.pd[:, 0, :], "pb" if j < 2 else "pd", "sm.X%d" % j, 256)
    wn, wk = window("sm", "O")
    cp("vs", T.go[:, 256:768], wn.indirect(T.l5[:, 16:48]), wk + " l5.R", "go.1", 55 + int(GATHER * 512))
    cp("vs", T.go[:, 768:V_], wn.indirect(T.l5[:, 48:80]), wk + " l5.R", "go.2", 55 + int(GATHER * 512))
    dma("y", T.goal[:, 256:V_], T.go[0:128:16, 256:V_], "go.1 go.2", "", LOAD)
    wn, wk = window("sm", "A")
    cp("vs", T.go[:, 0:256], wn.indirect(T.l5[:, 0:16]), wk + " l5.B", "go.0", 55 + int(GATHER * 256))
    dma("y", T.goal[:, 0:256], T.go[0:128:16, 0:256], "go.0", "", LOAD)
    emit(ops, eng, T)
